import numpy as np
import ml_dtypes


def mxq(x, axis, fmt="e4m3"):
    dtype, down = {"e4m3": (ml_dtypes.float8_e4m3fn, 7), "e5m2": (ml_dtypes.float8_e5m2, 14)}[fmt]
    v = np.moveaxis(np.asarray(x, np.float32).astype(ml_dtypes.bfloat16).astype(np.float64), axis, -1)
    blocks = v.reshape(v.shape[:-1] + (-1, 32))
    amax = np.abs(blocks).max(-1, keepdims=True)
    byte = np.maximum(np.where(amax > 0, np.frexp(amax)[1] - 1 + 127, 0) - down, 1)
    scale = np.exp2(byte - 127.0)
    codes = (blocks / scale).astype(np.float32).astype(dtype).astype(np.float64)
    return np.moveaxis((codes * scale).reshape(v.shape), -1, axis)


WIDE = False


def mx_kscale(k):
    if not WIDE:
        return np.ones(k)
    levels = np.array([10, -10, 5, -5, 0])
    if k % 512:
        return np.exp2(np.random.permutation(np.resize(levels, k // 32))).repeat(32)
    a = np.empty((k // 512, 16))
    for p in range(k // 512):
        a[p, :8] = np.random.permutation(np.resize(levels, 8))
        for g in range(8):
            far = levels[np.abs(levels - a[p, g]) >= 10]
            a[p, g + 8] = far[np.random.randint(len(far))]
    return np.exp2(a.ravel()).repeat(32)


BF16 = ml_dtypes.bfloat16


def bf(x):
    return np.asarray(x, np.float32).astype(BF16)


def f64(x):
    return np.asarray(x).astype(np.float64)


E2M1 = np.array([0.0, 0.5, 1.0, 1.5, 2.0, 3.0, 4.0, 6.0, -0.0, -0.5, -1.0, -1.5, -2.0, -3.0, -4.0, -6.0])


def pack_weight(w, fmt):
    k, n = w.shape
    w = f64(bf(w)).reshape(k // 32, 32, n)
    amax = np.abs(w).max(1)
    if fmt == "e4m3":
        byte = np.frexp(amax)[1] - 1 + 127 - 7
    else:
        mant, ex = np.frexp(amax / 6.0)
        byte = np.where(mant > 0.5, ex, ex - 1) + 127
    byte = np.clip(np.where(amax > 0, byte, 1), 1, 254)
    scaled = (w * np.exp2(127.0 - byte)[:, None, :]).reshape(k, n).astype(np.float32)
    by_word = np.ascontiguousarray(scaled.reshape(k // 512, 128, 4, n).transpose(0, 1, 3, 2))
    if fmt == "e4m3":
        words = by_word.astype(ml_dtypes.float8_e4m3fn).view(np.uint8)
    else:
        c = by_word.astype(ml_dtypes.float4_e2m1fn).view(np.uint8) & 0xF
        words = c[..., 0::2] | (c[..., 1::2] << 4)
    return np.ascontiguousarray(words), np.ascontiguousarray(byte.astype(np.uint8).reshape(k // 512, 16, n))


def unpack_weight(words, scales, fmt):
    g, p, n, _ = words.shape
    if fmt == "e4m3":
        vals = np.ascontiguousarray(words).view(ml_dtypes.float8_e4m3fn).astype(np.float64)
    else:
        nib = np.empty((g, p, n, 4), np.uint8)
        nib[..., 0::2] = words & 0xF
        nib[..., 1::2] = words >> 4
        vals = E2M1[nib]
    vals = vals * np.repeat(np.exp2(scales.astype(np.float64) - 127.0), 8, axis=1)[..., None]
    return vals.transpose(0, 1, 3, 2).reshape(g * 512, n)
def pack4(w):
    words, scales = pack_weight(w, "e2m1")
    return words.reshape(words.shape[0], 128, -1), scales


def unpack4(words, scales):
    return unpack_weight(words.reshape(words.shape[0], 128, -1, 2), scales, "e2m1")


def planes(Y):
    n, m = Y.shape
    b = f64(bf(Y)).reshape(n // 32, 32, m)
    amax = np.abs(b).max(1)
    byte = np.clip(np.where(amax > 0, np.frexp(amax)[1] - 1 + 127 - 7, 1), 1, 254)
    codes = (b * np.exp2(127.0 - byte)[:, None, :]).reshape(n, m).astype(np.float32).astype(ml_dtypes.float8_e4m3fn).view(np.uint8)
    words = codes.reshape(n // 512, 128, 4, m).transpose(0, 1, 3, 2)
    return np.ascontiguousarray(words), np.ascontiguousarray(byte.astype(np.uint8).reshape(n // 512, 16, m))


S, K, F = 1024, 1024, 1536


def setup_inputs():
    src = np.random.uniform(0.0, 2.0 * np.pi, S)
    acct = np.random.uniform(0.0, 2.0 * np.pi, K)
    mach = np.random.uniform(0.0, 2.0 * np.pi, F)
    s = mx_kscale(K)
    t = mx_kscale(F)
    X = np.random.rand(K, S) ** (5.0 - 4.0 * np.cos(acct[:, None] - src[None, :]))
    A = 0.8 / K * np.exp(np.random.randn(K, F) + 2.0 * np.cos(acct[:, None] - mach[None, :]) + 0.5 * np.random.randn(F))
    B = 0.27 / F * np.exp(np.random.randn(F, K) + 2.0 * np.cos(mach[:, None] - acct[None, :]) + 0.5 * np.random.randn(K))
    x_words, x_scales = pack_weight(X * s[:, None], "e4m3")
    a_words, a_scales = pack4(A / s[:, None])
    relay = bf(np.exp(0.5 * np.random.randn(F)) * t)
    b = bf(B / t[:, None])
    value = bf(np.exp(0.8 * np.random.randn(K)))
    return {"x_words": x_words, "x_scales": x_scales, "a_words": a_words, "a_scales": a_scales,
            "relay": relay, "b": b, "value": value}

def reference(x_words, x_scales, a_words, a_scales, relay, b, value):
    X = unpack_weight(x_words, x_scales, "e4m3")
    A = unpack4(a_words, a_scales)
    first = X.T @ A
    H = np.minimum(first, 1.0) * f64(relay)
    second = mxq(H, 1, "e4m3") @ mxq(f64(b), 0, "e4m3")
    y = np.minimum(second, 1.0) * f64(value)
    Y = y.T
    words, scales = planes(Y)
    return y, words, scales

@@ -1,0 +1,300 @@
+from contextlib import ExitStack
+
+import concourse.mybir as mybir
+from concourse.masks import make_identity
+
+S, K, F = 1024, 1024, 1536
+FLOPS = 2 * S * K * F * 2
+
+F32 = mybir.dt.float32
+BF16 = mybir.dt.bfloat16
+I32 = mybir.dt.int32
+U32 = mybir.dt.uint32
+U8 = mybir.dt.uint8
+FP8X4 = mybir.dt.float8_e4m3fn_x4
+FP4X4 = mybir.dt.float4_e2m1fn_x4
+MIN = mybir.AluOpType.min
+MULT = mybir.AluOpType.mult
+
+P = 128
+PASS = 512
+SLOTS = 4
+RUN = 8
+S_TILES = S // P
+K_PASSES = K // PASS
+F_PASSES = F // PASS
+X_CHUNKS = ((0, 128), (128, 384), (384, 1024))
+A_CHUNKS = ((0, 1), (1, 3))
+HEAD_JOBS, LEAD_PAIRS, BQ0, BQ1, BQ_STEP, LAG, TAIL, TAIL_LAG = 16, 2, 3, 13, 3, 5, 5, 2
+
+
+def pipeline(do):
+    first = [("s1", s, g) for s in range(S_TILES) for g in range(F_PASSES)]
+    pairs = [(j, 0) for j in range(LEAD_PAIRS)]
+    for j in range(S_TILES // 2):
+        pairs.append((j, 1))
+        if j + LEAD_PAIRS < S_TILES // 2:
+            pairs.append((j + LEAD_PAIRS, 0))
+    second = [("s2", 2 * j + i, h) for j, h in pairs for i in range(2)]
+    jobs = first[:HEAD_JOBS]
+    rest = first[HEAD_JOBS:]
+    for i, job in enumerate(second):
+        jobs.append(job)
+        jobs.extend(rest[i : i + 1])
+    n = len(jobs)
+
+    do["loads"]()
+    do["relay"]()
+    for g in range(F_PASSES):
+        do["perm"](g)
+    for h in range(K_PASSES):
+        for g in range(F_PASSES):
+            do["bi"](g, h)
+    bq_at = {}
+    for g in range(F_PASSES):
+        bq_at[BQ0 + BQ_STEP * g] = (g, 0)
+        bq_at[BQ1 + BQ_STEP * g] = (g, 1)
+    waiting, ready = [], []
+    tp_at, yq_at = {}, {}
+    for k in range(n + LAG + 4):
+        for group in tp_at.get(k, []):
+            do["tp"](*group)
+        for group in tp_at.get(k, []):
+            do["tev"](*group)
+        if 0 <= k - 1 < n:
+            kind, s, g = jobs[k - 1]
+            if kind == "s1":
+                do["hev"](s, g)
+            else:
+                do["yev"](s, g, k == n)
+                waiting.append(s)
+                if len(waiting) == 2 or k >= n - 1:
+                    ready.append((tuple(waiting), g))
+                    waiting = []
+                if len(ready) == 2 or (ready and k >= n - TAIL):
+                    at = max([k + (LAG if k < n - TAIL else TAIL_LAG)] + [t + 1 for t in tp_at])
+                    tp_at[at] = ready
+                    for i, group in enumerate(ready):
+                        yq_at.setdefault(at + 1 + i, []).append(group)
+                    ready = []
+        if 0 <= k - 2 < n and jobs[k - 2][0] == "s1":
+            do["hq"](*jobs[k - 2][1:])
+        for group in yq_at.get(k, []):
+            do["yq"](*group)
+        if k in bq_at:
+            do["bq"](*bq_at[k])
+        if k < n:
+            do[jobs[k][0]](*jobs[k][1:])
+
+
+def tile_clamped_two_hop_reach_h2_kernel(tc, x_words, x_scales, a_words, a_scales, relay, b, value, out_0, out_1, out_2):
+    nc = tc.nc
+    with ExitStack() as ctx:
+        keep = ctx.enter_context(tc.tile_pool(name="keep", bufs=1))
+        work = ctx.enter_context(tc.tile_pool(name="work", bufs=4))
+        psum = ctx.enter_context(tc.psum_pool(name="psum", bufs=1))
+        ctx.enter_context(tc.manual_schedule())
+
+        a_raw = [keep.tile([P, K_PASSES, 2 * PASS * (hi - lo)], U8, name="a_raw%d" % lo, align_bytes=64) for lo, hi in A_CHUNKS]
+        a_sc_raw = keep.tile([P, K_PASSES, F], U8, name="a_sc_raw", align_bytes=64)
+        a_codes = [keep.tile([P, K_PASSES, 2 * PASS], U8, name="a_codes%d" % g, align_bytes=64) for g in range(F_PASSES)]
+        a_sc = [keep.tile([P, K_PASSES, PASS], U8, name="a_sc%d" % g, align_bytes=64) for g in range(F_PASSES)]
+        x_codes = [keep.tile([P, K_PASSES, hi - lo], U32, name="x_codes%d" % lo, align_bytes=64) for lo, hi in X_CHUNKS]
+        x_sc = keep.tile([P, K_PASSES, S], U8, name="x_sc", align_bytes=64)
+        b_raw, b_codes, b_sc = {}, {}, {}
+        for g in range(F_PASSES):
+            for h in range(K_PASSES):
+                b_raw[g, h] = keep.tile([P, SLOTS, PASS], BF16, name="b_raw%d%d" % (g, h), align_bytes=64)
+                b_codes[g, h] = keep.tile([P, PASS], U32, name="b_codes%d%d" % (g, h), align_bytes=64)
+                b_sc[g, h] = keep.tile([P, PASS], U8, name="b_sc%d%d" % (g, h), align_bytes=64)
+        h_codes, h_sc = {}, {}
+        for s in range(S_TILES):
+            for g in range(F_PASSES):
+                h_codes[s, g] = keep.tile([P, P], U32, name="h_codes%d%d" % (s, g), align_bytes=64)
+                h_sc[s, g] = keep.tile([P, P], U8, name="h_sc%d%d" % (s, g), align_bytes=64)
+        y_codes = [keep.tile([P, S], U32, name="y_codes%d" % h, align_bytes=64) for h in range(K_PASSES)]
+        y_sc = [keep.tile([P, S], U8, name="y_sc%d" % h, align_bytes=64) for h in range(K_PASSES)]
+        relay_rows = keep.tile([P, F_PASSES * P], BF16, name="relay_rows", align_bytes=64)
+        relay_sb = keep.tile([P, F_PASSES, SLOTS], F32, name="relay_sb", align_bytes=64)
+        value_all = keep.tile([P, K], BF16, name="value_all", align_bytes=64)
+        ident_bf = keep.tile([P, P], BF16, name="ident_bf", align_bytes=64)
+        ident_f32 = keep.tile([P, P], F32, name="ident_f32", align_bytes=64)
+
+        acc, h_bf, b_int, y_bf, y_tp, y_t = {}, {}, {}, {}, {}, {}
+
+        def load_scale_rows(plane, rows):
+            for quad in range(4):
+                nc.sync.dma_start(
+                    out=plane[32 * quad : 32 * quad + 4, :, :].bitcast(I32),
+                    in_=rows[:, 4 * quad : 4 * quad + 4, :].rearrange("g r n -> r g n").bitcast(I32),
+                )
+
+        def load_x(c):
+            lo, hi = X_CHUNKS[c]
+            src = x_words.rearrange("g p n t -> p g (n t)").bitcast(I32)
+            nc.sync.dma_start(out=x_codes[c][:].bitcast(I32), in_=src[:, :, lo:hi])
+
+        def load_a(c):
+            lo, hi = A_CHUNKS[c]
+            src = a_words[:, :, 2 * PASS * lo : 2 * PASS * hi].rearrange("g p n -> p g n")
+            nc.sync.dma_start(out=a_raw[c][:].bitcast(I32), in_=src.bitcast(I32))
+
+        def load_b(g, h):
+            rows = b[PASS * g : PASS * (g + 1), PASS * h : PASS * (h + 1)].rearrange("(q t r) n -> t q r n", t=SLOTS, r=RUN)
+            for t in range(SLOTS):
+                nc.sync.dma_start(out=b_raw[g, h][:, t, :], in_=rows[t])
+
+        def loads():
+            nc.vector.memset(a_sc_raw[:].bitcast(I32), 0)
+            nc.vector.memset(x_sc[:].bitcast(I32), 0)
+            nc.gpsimd.memset(relay_rows[:], 0.0)
+            nc.gpsimd.dma_start(
+                out=relay_rows[0:SLOTS, :].rearrange("t (a r) -> t a r", r=RUN),
+                in_=relay.rearrange("(a t r) -> t a r", t=SLOTS, r=RUN),
+            )
+            make_identity(nc, ident_bf[:])
+            nc.scalar.copy(out=ident_f32[:], in_=ident_bf[:])
+            load_a(0)
+            load_x(0)
+            load_scale_rows(a_sc_raw, a_scales)
+            load_scale_rows(x_sc, x_scales)
+            load_a(1)
+            load_b(0, 0)
+            load_x(1)
+            load_b(1, 0)
+            load_b(2, 0)
+            load_x(2)
+            nc.sync.dma_start(out=value_all[:], in_=value.partition_broadcast(P))
+            for g in range(F_PASSES):
+                load_b(g, 1)
+
+        def turn_relay():
+            turned = psum.tile([P, F_PASSES, P], BF16, name="turned", tag="tp", bufs=2)
+            for g in range(F_PASSES):
+                nc.tensor.transpose(turned[:, g, :], relay_rows[:, P * g : P * (g + 1)], ident_bf[:])
+            nc.scalar.copy(out=relay_sb[:], in_=turned[:, :, 0:SLOTS])
+
+        def perm(g):
+            c = [i for i, (lo, hi) in enumerate(A_CHUNKS) if lo <= g < hi][0]
+            for dst, src, per_col, at in ((a_codes[g], a_raw[c], 2, g - A_CHUNKS[c][0]), (a_sc[g], a_sc_raw, 1, g)):
+                w = RUN * per_col // 4
+                nc.vector.tensor_copy(
+                    out=dst[:].bitcast(I32).rearrange("p k (t q w) -> p k t q w", t=SLOTS, w=w),
+                    in_=src[:, :, per_col * PASS * at : per_col * PASS * (at + 1)].bitcast(I32).rearrange("p k (q t w) -> p k t q w", t=SLOTS, w=w),
+                )
+
+        def s1(s, g):
+            bank = psum.tile([P, SLOTS, P], F32, name="acc1", tag="acc", bufs=6)
+            acc[s, g, 1] = bank
+            c = [i for i, (lo, hi) in enumerate(X_CHUNKS) if lo <= P * s < hi][0]
+            off = P * s - X_CHUNKS[c][0]
+            for t in range(SLOTS):
+                for k in range(K_PASSES):
+                    nc.tensor.matmul_mx(
+                        out=bank[:, t, :],
+                        lhsT=a_codes[g][:, k, 2 * P * t : 2 * P * (t + 1)].bitcast(FP4X4),
+                        lhsT_scale=a_sc[g][:, k, P * t : P * (t + 1)],
+                        rhs=x_codes[c][:, k, off : off + P].bitcast(FP8X4),
+                        rhs_scale=x_sc[:, k, P * s : P * (s + 1)],
+                        start=(k == 0),
+                        stop=(k == K_PASSES - 1),
+                    )
+
+        def hev(s, g):
+            tile_bf = work.tile([P, P, SLOTS], BF16, name="h_bf", tag="h_bf", bufs=4, align_bytes=64)
+            h_bf[s, g] = tile_bf
+            nc.vector.scalar_tensor_tensor(
+                out=tile_bf[:],
+                in0=acc[s, g, 1][:].rearrange("p t s -> p s t"),
+                scalar=1.0,
+                in1=relay_sb[:, g : g + 1, :].to_broadcast([P, P, SLOTS]),
+                op0=MIN,
+                op1=MULT,
+            )
+
+        def hq(s, g):
+            nc.vector.quantize_mx(
+                out=h_codes[s, g][:].bitcast(FP8X4), scales=h_sc[s, g][:], in_=h_bf[s, g][:].rearrange("p s t -> p (s t)")
+            )
+
+        def bi(g, h):
+            tile_bf = work.tile([P, PASS, SLOTS], BF16, name="b_int", tag="b_int", bufs=6, align_bytes=64)
+            b_int[g, h] = tile_bf
+            nc.scalar.copy(
+                out=tile_bf[:].rearrange("p (c i) t -> p c t i", i=4),
+                in_=b_raw[g, h][:].rearrange("p t (c i) -> p c t i", i=4),
+            )
+
+        def bq(g, h):
+            nc.vector.quantize_mx(
+                out=b_codes[g, h][:].bitcast(FP8X4), scales=b_sc[g, h][:], in_=b_int[g, h][:].rearrange("p n t -> p (n t)")
+            )
+
+        def s2(s, h):
+            bank = psum.tile([P, PASS], F32, name="acc2", tag="acc", bufs=6)
+            acc[s, h, 2] = bank
+            for g in range(F_PASSES):
+                nc.tensor.matmul_mx(
+                    out=bank[:],
+                    lhsT=h_codes[s, g][:].bitcast(FP8X4),
+                    lhsT_scale=h_sc[s, g][:],
+                    rhs=b_codes[g, h][:].bitcast(FP8X4),
+                    rhs_scale=b_sc[g, h][:],
+                    start=(g == 0),
+                    stop=(g == F_PASSES - 1),
+                )
+
+        def yev(s, h, last):
+            cols = slice(PASS * h, PASS * (h + 1))
+            y32 = work.tile([P, PASS], F32, name="y32", tag="y32", bufs=6, align_bytes=64)
+            tile_bf = work.tile([P, PASS], BF16, name="y_bf", tag="y_bf", bufs=8, align_bytes=64)
+            y_bf[s, h] = tile_bf
+            sorted_bf = tile_bf[:].rearrange("s (u p e) -> s u p e", u=2, e=2)
+            if last:
+                sums = acc[s, h, 2][:].rearrange("s (p u e) -> s u p e", u=2, e=2)
+                gains = value_all[:, cols].rearrange("s (p u e) -> s u p e", u=2, e=2)
+                for u in range(2):
+                    nc.vector.scalar_tensor_tensor(
+                        out=sorted_bf[:, u], in0=sums[:, u], scalar=1.0, in1=gains[:, u], op0=MIN, op1=MULT
+                    )
+            nc.vector.scalar_tensor_tensor(
+                out=y32[:], in0=acc[s, h, 2][:], scalar=1.0, in1=value_all[:, cols], op0=MIN, op1=MULT
+            )
+            if not last:
+                nc.scalar.copy(out=sorted_bf, in_=y32[:].rearrange("s (p u e) -> s u p e", u=2, e=2))
+            nc.sync.dma_start(out=out_0[P * s : P * (s + 1), cols], in_=y32[:])
+
+        def tp(tiles, h):
+            bank = psum.tile([P, len(tiles), 2, P], F32, name="turned", tag="tp", bufs=2)
+            y_tp[tiles, h] = bank
+            for i, s in enumerate(tiles):
+                words = y_bf[s, h][:].bitcast(F32)
+                for u in range(2):
+                    nc.tensor.transpose(bank[:, i, u, :], words[:, P * u : P * (u + 1)], ident_f32[:])
+
+        def tev(tiles, h):
+            tile_bf = work.tile([P, len(tiles) * PASS], BF16, name="y_t", tag="y_t", bufs=4, align_bytes=64)
+            y_t[tiles, h] = tile_bf
+            nc.scalar.copy(
+                out=tile_bf[:].bitcast(F32).rearrange("p (i s u) -> p i s u", s=P, u=2),
+                in_=y_tp[tiles, h][:].rearrange("p i u s -> p i s u"),
+            )
+
+        def yq(tiles, h):
+            cols = slice(P * tiles[0], P * (tiles[-1] + 1))
+            nc.vector.quantize_mx(out=y_codes[h][:, cols].bitcast(FP8X4), scales=y_sc[h][:, cols], in_=y_t[tiles, h][:])
+            words = out_1[h].rearrange("p m t -> p (m t)").bitcast(I32)
+            nc.sync.dma_start(out=words[:, cols], in_=y_codes[h][:, cols].bitcast(I32))
+            if tiles[-1] == S_TILES - 1:
+                for quad in range(4):
+                    nc.sync.dma_start(
+                        out=out_2[h, 4 * quad : 4 * quad + 4, :].bitcast(I32),
+                        in_=y_sc[h][32 * quad : 32 * quad + 4, :].bitcast(I32),
+                    )
+
+        pipeline(
+            {
+                "loads": loads, "relay": turn_relay, "perm": perm, "bi": bi, "bq": bq, "s1": s1, "hev": hev, "hq": hq,
+                "s2": s2, "yev": yev, "tp": tp, "tev": tev, "yq": yq,
+            }
+        )

@@ -23,66 +23,76 @@ RUN = 8
 S_TILES = S // P
 K_PASSES = K // PASS
 F_PASSES = F // PASS
-X_CHUNKS = ((0, 128), (128, 384), (384, 1024))
+WIDE = 256
+RANGES = ((0, 256), (256, 512), (512, 768), (768, 1024))
 A_CHUNKS = ((0, 1), (1, 3))
-HEAD_JOBS, LEAD_PAIRS, BQ0, BQ1, BQ_STEP, LAG, TAIL, TAIL_LAG = 16, 2, 3, 13, 3, 5, 5, 2
+HEAD, LEAD, LAG, TAIL, TAIL_LAG, BATCH = 18, 2, 4, 5, 2, 2
+B0, BS, B1, BS1, BQL, HQL, HQL2 = 0, 3, 9, 4, 6, 6, 3
+LOADS = (("a", 0), ("x", 0), ("asc",), ("xsc",), ("a", 1), ("b", 0, 0), ("x", 1), ("b", 1, 0), ("b", 2, 0), ("x", 2), ("b", 0, 1), ("x", 3), ("b", 1, 1), ("b", 2, 1), ("value",))
 
 
 def pipeline(do):
-    first = [("s1", s, g) for s in range(S_TILES) for g in range(F_PASSES)]
-    pairs = [(j, 0) for j in range(LEAD_PAIRS)]
+    first = []
+    for r, (lo, hi) in enumerate(RANGES):
+        for g in range(F_PASSES):
+            first.extend([("s1", r, g, j) for j in range((hi - lo) // P)])
+    pairs = [(j, 0) for j in range(LEAD)]
     for j in range(S_TILES // 2):
         pairs.append((j, 1))
-        if j + LEAD_PAIRS < S_TILES // 2:
-            pairs.append((j + LEAD_PAIRS, 0))
+        if j + LEAD < S_TILES // 2:
+            pairs.append((j + LEAD, 0))
     second = [("s2", 2 * j + i, h) for j, h in pairs for i in range(2)]
-    jobs = first[:HEAD_JOBS]
-    rest = first[HEAD_JOBS:]
+    jobs = first[:HEAD]
+    rest = first[HEAD:]
     for i, job in enumerate(second):
         jobs.append(job)
         jobs.extend(rest[i : i + 1])
     n = len(jobs)
-
-    do["loads"]()
+    do["setup"]()
+    for l in LOADS:
+        do["load"](*l)
     do["relay"]()
     for g in range(F_PASSES):
         do["perm"](g)
-    for h in range(K_PASSES):
-        for g in range(F_PASSES):
-            do["bi"](g, h)
-    bq_at = {}
-    for g in range(F_PASSES):
-        bq_at[BQ0 + BQ_STEP * g] = (g, 0)
-        bq_at[BQ1 + BQ_STEP * g] = (g, 1)
+    b_at = {B0: (0, 0), B0 + BS: (1, 0), B0 + 2 * BS: (2, 0), B1: (0, 1), B1 + BS1: (1, 1), B1 + 2 * BS1: (2, 1)}
     waiting, ready = [], []
-    tp_at, yq_at = {}, {}
+    tp_at, yq_at, hq_at = {}, {}, {}
     for k in range(n + LAG + 4):
         for group in tp_at.get(k, []):
             do["tp"](*group)
         for group in tp_at.get(k, []):
             do["tev"](*group)
+        if k in b_at:
+            do["bi"](*b_at[k])
+        if k - BQL in b_at:
+            do["bq"](*b_at[k - BQL])
+        if k in hq_at:
+            do["hq"](*hq_at[k])
         if 0 <= k - 1 < n:
-            kind, s, g = jobs[k - 1]
-            if kind == "s1":
-                do["hev"](s, g)
+            job = jobs[k - 1]
+            if job[0] == "s1":
+                do["hev"](*job[1:])
+                r, g, j = job[1:]
+                if j == (RANGES[r][1] - RANGES[r][0]) // P - 1:
+                    do["hi"](r, g)
+                    hq_at[k + (HQL if k < HEAD + 2 else HQL2)] = (r, g)
             else:
+                s, g = job[1:]
                 do["yev"](s, g, k == n)
+                if k != n:
+                    do["cast"](s, g)
                 waiting.append(s)
                 if len(waiting) == 2 or k >= n - 1:
                     ready.append((tuple(waiting), g))
                     waiting = []
-                if len(ready) == 2 or (ready and k >= n - TAIL):
+                if len(ready) == BATCH or (ready and k >= n - TAIL):
                     at = max([k + (LAG if k < n - TAIL else TAIL_LAG)] + [t + 1 for t in tp_at])
                     tp_at[at] = ready
                     for i, group in enumerate(ready):
                         yq_at.setdefault(at + 1 + i, []).append(group)
                     ready = []
-        if 0 <= k - 2 < n and jobs[k - 2][0] == "s1":
-            do["hq"](*jobs[k - 2][1:])
         for group in yq_at.get(k, []):
             do["yq"](*group)
-        if k in bq_at:
-            do["bq"](*bq_at[k])
         if k < n:
             do[jobs[k][0]](*jobs[k][1:])
 
@@ -99,7 +109,7 @@ def tile_clamped_two_hop_reach_h2_kernel(tc, x_words, x_scales, a_words, a_scale
         a_sc_raw = keep.tile([P, K_PASSES, F], U8, name="a_sc_raw", align_bytes=64)
         a_codes = [keep.tile([P, K_PASSES, 2 * PASS], U8, name="a_codes%d" % g, align_bytes=64) for g in range(F_PASSES)]
         a_sc = [keep.tile([P, K_PASSES, PASS], U8, name="a_sc%d" % g, align_bytes=64) for g in range(F_PASSES)]
-        x_codes = [keep.tile([P, K_PASSES, hi - lo], U32, name="x_codes%d" % lo, align_bytes=64) for lo, hi in X_CHUNKS]
+        x_codes = [keep.tile([P, K_PASSES, hi - lo], U32, name="x_codes%d" % lo, align_bytes=64) for lo, hi in RANGES]
         x_sc = keep.tile([P, K_PASSES, S], U8, name="x_sc", align_bytes=64)
         b_raw, b_codes, b_sc = {}, {}, {}
         for g in range(F_PASSES):
@@ -108,10 +118,10 @@ def tile_clamped_two_hop_reach_h2_kernel(tc, x_words, x_scales, a_words, a_scale
                 b_codes[g, h] = keep.tile([P, PASS], U32, name="b_codes%d%d" % (g, h), align_bytes=64)
                 b_sc[g, h] = keep.tile([P, PASS], U8, name="b_sc%d%d" % (g, h), align_bytes=64)
         h_codes, h_sc = {}, {}
-        for s in range(S_TILES):
+        for r in range(len(RANGES)):
             for g in range(F_PASSES):
-                h_codes[s, g] = keep.tile([P, P], U32, name="h_codes%d%d" % (s, g), align_bytes=64)
-                h_sc[s, g] = keep.tile([P, P], U8, name="h_sc%d%d" % (s, g), align_bytes=64)
+                h_codes[r, g] = keep.tile([P, WIDE], U32, name="h_codes%d%d" % (r, g), align_bytes=64)
+                h_sc[r, g] = keep.tile([P, WIDE], U8, name="h_sc%d%d" % (r, g), align_bytes=64)
         y_codes = [keep.tile([P, S], U32, name="y_codes%d" % h, align_bytes=64) for h in range(K_PASSES)]
         y_sc = [keep.tile([P, S], U8, name="y_sc%d" % h, align_bytes=64) for h in range(K_PASSES)]
         relay_rows = keep.tile([P, F_PASSES * P], BF16, name="relay_rows", align_bytes=64)
@@ -120,7 +130,7 @@ def tile_clamped_two_hop_reach_h2_kernel(tc, x_words, x_scales, a_words, a_scale
         ident_bf = keep.tile([P, P], BF16, name="ident_bf", align_bytes=64)
         ident_f32 = keep.tile([P, P], F32, name="ident_f32", align_bytes=64)
 
-        acc, h_bf, b_int, y_bf, y_tp, y_t = {}, {}, {}, {}, {}, {}
+        acc, h_pairs, h_bf, b_int, y_f32, y_bf, y_tp, y_t = {}, {}, {}, {}, {}, {}, {}, {}
 
         def load_scale_rows(plane, rows):
             for quad in range(4):
@@ -130,7 +140,7 @@ def tile_clamped_two_hop_reach_h2_kernel(tc, x_words, x_scales, a_words, a_scale
                 )
 
         def load_x(c):
-            lo, hi = X_CHUNKS[c]
+            lo, hi = RANGES[c]
             src = x_words.rearrange("g p n t -> p g (n t)").bitcast(I32)
             nc.sync.dma_start(out=x_codes[c][:].bitcast(I32), in_=src[:, :, lo:hi])
 
@@ -144,7 +154,7 @@ def tile_clamped_two_hop_reach_h2_kernel(tc, x_words, x_scales, a_words, a_scale
             for t in range(SLOTS):
                 nc.sync.dma_start(out=b_raw[g, h][:, t, :], in_=rows[t])
 
-        def loads():
+        def setup():
             nc.vector.memset(a_sc_raw[:].bitcast(I32), 0)
             nc.vector.memset(x_sc[:].bitcast(I32), 0)
             nc.gpsimd.memset(relay_rows[:], 0.0)
@@ -154,19 +164,20 @@ def tile_clamped_two_hop_reach_h2_kernel(tc, x_words, x_scales, a_words, a_scale
             )
             make_identity(nc, ident_bf[:])
             nc.scalar.copy(out=ident_f32[:], in_=ident_bf[:])
-            load_a(0)
-            load_x(0)
-            load_scale_rows(a_sc_raw, a_scales)
-            load_scale_rows(x_sc, x_scales)
-            load_a(1)
-            load_b(0, 0)
-            load_x(1)
-            load_b(1, 0)
-            load_b(2, 0)
-            load_x(2)
-            nc.sync.dma_start(out=value_all[:], in_=value.partition_broadcast(P))
-            for g in range(F_PASSES):
-                load_b(g, 1)
+
+        def load(kind, *at):
+            if kind == "a":
+                load_a(*at)
+            elif kind == "x":
+                load_x(*at)
+            elif kind == "b":
+                load_b(*at)
+            elif kind == "asc":
+                load_scale_rows(a_sc_raw, a_scales)
+            elif kind == "xsc":
+                load_scale_rows(x_sc, x_scales)
+            else:
+                nc.sync.dma_start(out=value_all[:], in_=value.partition_broadcast(P))
 
         def turn_relay():
             turned = psum.tile([P, F_PASSES, P], BF16, name="turned", tag="tp", bufs=2)
@@ -183,39 +194,45 @@ def tile_clamped_two_hop_reach_h2_kernel(tc, x_words, x_scales, a_words, a_scale
                     in_=src[:, :, per_col * PASS * at : per_col * PASS * (at + 1)].bitcast(I32).rearrange("p k (q t w) -> p k t q w", t=SLOTS, w=w),
                 )
 
-        def s1(s, g):
-            bank = psum.tile([P, SLOTS, P], F32, name="acc1", tag="acc", bufs=6)
-            acc[s, g, 1] = bank
-            c = [i for i, (lo, hi) in enumerate(X_CHUNKS) if lo <= P * s < hi][0]
-            off = P * s - X_CHUNKS[c][0]
-            for t in range(SLOTS):
-                for k in range(K_PASSES):
-                    nc.tensor.matmul_mx(
-                        out=bank[:, t, :],
-                        lhsT=a_codes[g][:, k, 2 * P * t : 2 * P * (t + 1)].bitcast(FP4X4),
-                        lhsT_scale=a_sc[g][:, k, P * t : P * (t + 1)],
-                        rhs=x_codes[c][:, k, off : off + P].bitcast(FP8X4),
-                        rhs_scale=x_sc[:, k, P * s : P * (s + 1)],
-                        start=(k == 0),
-                        stop=(k == K_PASSES - 1),
-                    )
+        def s1(r, g, u):
+            bank = psum.tile([P, 2, WIDE], F32, name="acc1", tag="acc", bufs=6)
+            acc[r, g, u, 1] = bank
+            for e in range(2):
+                t = 2 * u + e
+                for off in range(0, WIDE, P):
+                    for k in range(K_PASSES):
+                        nc.tensor.matmul_mx(
+                            out=bank[:, e, off : off + P],
+                            lhsT=a_codes[g][:, k, 2 * P * t : 2 * P * (t + 1)].bitcast(FP4X4),
+                            lhsT_scale=a_sc[g][:, k, P * t : P * (t + 1)],
+                            rhs=x_codes[r][:, k, off : off + P].bitcast(FP8X4),
+                            rhs_scale=x_sc[:, k, WIDE * r + off : WIDE * r + off + P],
+                            start=(k == 0),
+                            stop=(k == K_PASSES - 1),
+                        )
 
-        def hev(s, g):
-            tile_bf = work.tile([P, P, SLOTS], BF16, name="h_bf", tag="h_bf", bufs=4, align_bytes=64)
-            h_bf[s, g] = tile_bf
+        def hev(r, g, u):
+            if u == 0:
+                h_pairs[r, g] = work.tile([P, SLOTS * WIDE], BF16, name="h_pairs", tag="h_pairs", bufs=4, align_bytes=64)
             nc.vector.scalar_tensor_tensor(
-                out=tile_bf[:],
-                in0=acc[s, g, 1][:].rearrange("p t s -> p s t"),
+                out=h_pairs[r, g][:, 2 * WIDE * u : 2 * WIDE * (u + 1)].rearrange("p (s e) -> p s e", e=2),
+                in0=acc[r, g, u, 1][:].rearrange("p e s -> p s e"),
                 scalar=1.0,
-                in1=relay_sb[:, g : g + 1, :].to_broadcast([P, P, SLOTS]),
+                in1=relay_sb[:, g : g + 1, 2 * u : 2 * u + 2].to_broadcast([P, WIDE, 2]),
                 op0=MIN,
                 op1=MULT,
             )
 
-        def hq(s, g):
-            nc.vector.quantize_mx(
-                out=h_codes[s, g][:].bitcast(FP8X4), scales=h_sc[s, g][:], in_=h_bf[s, g][:].rearrange("p s t -> p (s t)")
+        def hi(r, g):
+            tile_bf = work.tile([P, SLOTS * WIDE], BF16, name="h_bf", tag="h_bf", bufs=5, align_bytes=64)
+            h_bf[r, g] = tile_bf
+            nc.scalar.copy(
+                out=tile_bf[:].bitcast(F32).rearrange("p (s u) -> p s u", u=2),
+                in_=h_pairs[r, g][:].bitcast(F32).rearrange("p (u s) -> p s u", u=2),
             )
+
+        def hq(r, g):
+            nc.vector.quantize_mx(out=h_codes[r, g][:].bitcast(FP8X4), scales=h_sc[r, g][:], in_=h_bf[r, g][:])
 
         def bi(g, h):
             tile_bf = work.tile([P, PASS, SLOTS], BF16, name="b_int", tag="b_int", bufs=6, align_bytes=64)
@@ -233,11 +250,12 @@ def tile_clamped_two_hop_reach_h2_kernel(tc, x_words, x_scales, a_words, a_scale
         def s2(s, h):
             bank = psum.tile([P, PASS], F32, name="acc2", tag="acc", bufs=6)
             acc[s, h, 2] = bank
+            r, off = divmod(P * s, WIDE)
             for g in range(F_PASSES):
                 nc.tensor.matmul_mx(
                     out=bank[:],
-                    lhsT=h_codes[s, g][:].bitcast(FP8X4),
-                    lhsT_scale=h_sc[s, g][:],
+                    lhsT=h_codes[r, g][:, off : off + P].bitcast(FP8X4),
+                    lhsT_scale=h_sc[r, g][:, off : off + P],
                     rhs=b_codes[g, h][:].bitcast(FP8X4),
                     rhs_scale=b_sc[g, h][:],
                     start=(g == 0),
@@ -260,9 +278,14 @@ def tile_clamped_two_hop_reach_h2_kernel(tc, x_words, x_scales, a_words, a_scale
             nc.vector.scalar_tensor_tensor(
                 out=y32[:], in0=acc[s, h, 2][:], scalar=1.0, in1=value_all[:, cols], op0=MIN, op1=MULT
             )
-            if not last:
-                nc.scalar.copy(out=sorted_bf, in_=y32[:].rearrange("s (p u e) -> s u p e", u=2, e=2))
+            y_f32[s, h] = y32
             nc.sync.dma_start(out=out_0[P * s : P * (s + 1), cols], in_=y32[:])
+
+        def cast(s, h):
+            nc.scalar.copy(
+                out=y_bf[s, h][:].rearrange("s (u p e) -> s u p e", u=2, e=2),
+                in_=y_f32[s, h][:].rearrange("s (p u e) -> s u p e", u=2, e=2),
+            )
 
         def tp(tiles, h):
             bank = psum.tile([P, len(tiles), 2, P], F32, name="turned", tag="tp", bufs=2)
@@ -294,7 +317,7 @@ def tile_clamped_two_hop_reach_h2_kernel(tc, x_words, x_scales, a_words, a_scale
 
         pipeline(
             {
-                "loads": loads, "relay": turn_relay, "perm": perm, "bi": bi, "bq": bq, "s1": s1, "hev": hev, "hq": hq,
+                "setup": setup, "load": load, "hi": hi, "cast": cast, "relay": turn_relay, "perm": perm, "bi": bi, "bq": bq, "s1": s1, "hev": hev, "hq": hq,
                 "s2": s2, "yev": yev, "tp": tp, "tev": tev, "yq": yq,
             }
         )

@@ -155,10 +155,10 @@ def tile_clamped_two_hop_reach_h2_kernel(tc, x_words, x_scales, a_words, a_scale
                 nc.sync.dma_start(out=b_raw[g, h][:, t, :], in_=rows[t])
 
         def setup():
+            nc.vector.memset(relay_rows[:], 0.0)
             nc.vector.memset(a_sc_raw[:].bitcast(I32), 0)
             nc.vector.memset(x_sc[:].bitcast(I32), 0)
-            nc.gpsimd.memset(relay_rows[:], 0.0)
-            nc.gpsimd.dma_start(
+            nc.scalar.dma_start(
                 out=relay_rows[0:SLOTS, :].rearrange("t (a r) -> t a r", r=RUN),
                 in_=relay.rearrange("(a t r) -> t a r", t=SLOTS, r=RUN),
             )
@@ -194,15 +194,17 @@ def tile_clamped_two_hop_reach_h2_kernel(tc, x_words, x_scales, a_words, a_scale
                     in_=src[:, :, per_col * PASS * at : per_col * PASS * (at + 1)].bitcast(I32).rearrange("p k (q t w) -> p k t q w", t=SLOTS, w=w),
                 )
 
-        def s1(r, g, u):
-            bank = psum.tile([P, 2, WIDE], F32, name="acc1", tag="acc", bufs=6)
-            acc[r, g, u, 1] = bank
-            for e in range(2):
-                t = 2 * u + e
-                for off in range(0, WIDE, P):
-                    for k in range(K_PASSES):
+        def s1(r, g, j):
+            if j > 0:
+                return
+            for i in range(WIDE // P):
+                acc[r, g, i, 1] = psum.tile([P, SLOTS, P], F32, name="acc1", tag="acc", bufs=6)
+            for t in range(SLOTS):
+                for k in range(K_PASSES):
+                    for i in range(WIDE // P):
+                        off = P * i
                         nc.tensor.matmul_mx(
-                            out=bank[:, e, off : off + P],
+                            out=acc[r, g, i, 1][:, t, :],
                             lhsT=a_codes[g][:, k, 2 * P * t : 2 * P * (t + 1)].bitcast(FP4X4),
                             lhsT_scale=a_sc[g][:, k, P * t : P * (t + 1)],
                             rhs=x_codes[r][:, k, off : off + P].bitcast(FP8X4),
@@ -211,17 +213,19 @@ def tile_clamped_two_hop_reach_h2_kernel(tc, x_words, x_scales, a_words, a_scale
                             stop=(k == K_PASSES - 1),
                         )
 
-        def hev(r, g, u):
-            if u == 0:
+        def hev(r, g, i):
+            if i == 0:
                 h_pairs[r, g] = work.tile([P, SLOTS * WIDE], BF16, name="h_pairs", tag="h_pairs", bufs=4, align_bytes=64)
-            nc.vector.scalar_tensor_tensor(
-                out=h_pairs[r, g][:, 2 * WIDE * u : 2 * WIDE * (u + 1)].rearrange("p (s e) -> p s e", e=2),
-                in0=acc[r, g, u, 1][:].rearrange("p e s -> p s e"),
-                scalar=1.0,
-                in1=relay_sb[:, g : g + 1, 2 * u : 2 * u + 2].to_broadcast([P, WIDE, 2]),
-                op0=MIN,
-                op1=MULT,
-            )
+            for u in range(2):
+                at = 2 * (WIDE * u + P * i)
+                nc.vector.scalar_tensor_tensor(
+                    out=h_pairs[r, g][:, at : at + 2 * P].rearrange("p (s e) -> p s e", e=2),
+                    in0=acc[r, g, i, 1][:, 2 * u : 2 * u + 2, :].rearrange("p e s -> p s e"),
+                    scalar=1.0,
+                    in1=relay_sb[:, g : g + 1, 2 * u : 2 * u + 2].to_broadcast([P, P, 2]),
+                    op0=MIN,
+                    op1=MULT,
+                )
 
         def hi(r, g):
             tile_bf = work.tile([P, SLOTS * WIDE], BF16, name="h_bf", tag="h_bf", bufs=5, align_bytes=64)
@@ -288,7 +292,10 @@ def tile_clamped_two_hop_reach_h2_kernel(tc, x_words, x_scales, a_words, a_scale
             )
 
         def tp(tiles, h):
-            bank = psum.tile([P, len(tiles), 2, P], F32, name="turned", tag="tp", bufs=2)
+            if len(tiles) == 2:
+                bank = psum.tile([P, 2, 2, P], F32, name="turned", tag="tp", bufs=2)
+            else:
+                bank = psum.tile([P, 1, 2, P], F32, name="turned_last", tag="acc", bufs=6)
             y_tp[tiles, h] = bank
             for i, s in enumerate(tiles):
                 words = y_bf[s, h][:].bitcast(F32)

from contextlib import ExitStack

import concourse.mybir as mybir
from concourse.masks import make_identity

S, K, F = 1024, 1024, 1536
FLOPS = 2 * S * K * F * 2

F32 = mybir.dt.float32
BF16 = mybir.dt.bfloat16
I32 = mybir.dt.int32
U32 = mybir.dt.uint32
U8 = mybir.dt.uint8
FP8X4 = mybir.dt.float8_e4m3fn_x4
FP4X4 = mybir.dt.float4_e2m1fn_x4
MIN = mybir.AluOpType.min
MULT = mybir.AluOpType.mult

P = 128
PASS = 512
SLOTS = 4
RUN = 8
S_TILES = S // P
K_PASSES = K // PASS
F_PASSES = F // PASS
WIDE = 256
RANGES = ((0, 256), (256, 512), (512, 768), (768, 1024))
A_CHUNKS = ((0, 1), (1, 3))
HEAD, LEAD, LAG, TAIL, TAIL_LAG, BATCH = 18, 2, 4, 5, 2, 2
B0, BS, B1, BS1, BQL, HQL, HQL2 = 0, 3, 9, 4, 6, 6, 3
LOADS = (("a", 0), ("x", 0), ("asc",), ("xsc",), ("a", 1), ("b", 0, 0), ("x", 1), ("b", 1, 0), ("b", 2, 0), ("x", 2), ("b", 0, 1), ("x", 3), ("b", 1, 1), ("b", 2, 1), ("value",))


def pipeline(do):
    first = []
    for r, (lo, hi) in enumerate(RANGES):
        for g in range(F_PASSES):
            first.extend([("s1", r, g, j) for j in range((hi - lo) // P)])
    pairs = [(j, 0) for j in range(LEAD)]
    for j in range(S_TILES // 2):
        pairs.append((j, 1))
        if j + LEAD < S_TILES // 2:
            pairs.append((j + LEAD, 0))
    second = [("s2", 2 * j + i, h) for j, h in pairs for i in range(2)]
    jobs = first[:HEAD]
    rest = first[HEAD:]
    for i, job in enumerate(second):
        jobs.append(job)
        jobs.extend(rest[i : i + 1])
    n = len(jobs)
    do["setup"]()
    for l in LOADS:
        do["load"](*l)
    do["relay"]()
    for g in range(F_PASSES):
        do["perm"](g)
    b_at = {B0: (0, 0), B0 + BS: (1, 0), B0 + 2 * BS: (2, 0), B1: (0, 1), B1 + BS1: (1, 1), B1 + 2 * BS1: (2, 1)}
    waiting, ready = [], []
    tp_at, yq_at, hq_at = {}, {}, {}
    for k in range(n + LAG + 4):
        for group in tp_at.get(k, []):
            do["tp"](*group)
        for group in tp_at.get(k, []):
            do["tev"](*group)
        if k in b_at:
            do["bi"](*b_at[k])
        if k - BQL in b_at:
            do["bq"](*b_at[k - BQL])
        if k in hq_at:
            do["hq"](*hq_at[k])
        if 0 <= k - 1 < n:
            job = jobs[k - 1]
            if job[0] == "s1":
                do["hev"](*job[1:])
                r, g, j = job[1:]
                if j == (RANGES[r][1] - RANGES[r][0]) // P - 1:
                    do["hi"](r, g)
                    hq_at[k + (HQL if k < HEAD + 2 else HQL2)] = (r, g)
            else:
                s, g = job[1:]
                do["yev"](s, g, k == n)
                if k != n:
                    do["cast"](s, g)
                waiting.append(s)
                if len(waiting) == 2 or k >= n - 1:
                    ready.append((tuple(waiting), g))
                    waiting = []
                if len(ready) == BATCH or (ready and k >= n - TAIL):
                    at = max([k + (LAG if k < n - TAIL else TAIL_LAG)] + [t + 1 for t in tp_at])
                    tp_at[at] = ready
                    for i, group in enumerate(ready):
                        yq_at.setdefault(at + 1 + i, []).append(group)
                    ready = []
        for group in yq_at.get(k, []):
            do["yq"](*group)
        if k < n:
            do[jobs[k][0]](*jobs[k][1:])


def tile_clamped_two_hop_reach_h2_kernel(tc, x_words, x_scales, a_words, a_scales, relay, b, value, out_0, out_1, out_2):
    nc = tc.nc
    with ExitStack() as ctx:
        keep = ctx.enter_context(tc.tile_pool(name="keep", bufs=1))
        work = ctx.enter_context(tc.tile_pool(name="work", bufs=4))
        psum = ctx.enter_context(tc.psum_pool(name="psum", bufs=1))
        ctx.enter_context(tc.manual_schedule())

        a_raw = [keep.tile([P, K_PASSES, 2 * PASS * (hi - lo)], U8, name="a_raw%d" % lo, align_bytes=64) for lo, hi in A_CHUNKS]
        a_sc_raw = keep.tile([P, K_PASSES, F], U8, name="a_sc_raw", align_bytes=64)
        a_codes = [keep.tile([P, K_PASSES, 2 * PASS], U8, name="a_codes%d" % g, align_bytes=64) for g in range(F_PASSES)]
        a_sc = [keep.tile([P, K_PASSES, PASS], U8, name="a_sc%d" % g, align_bytes=64) for g in range(F_PASSES)]
        x_codes = [keep.tile([P, K_PASSES, hi - lo], U32, name="x_codes%d" % lo, align_bytes=64) for lo, hi in RANGES]
        x_sc = keep.tile([P, K_PASSES, S], U8, name="x_sc", align_bytes=64)
        b_raw, b_codes, b_sc = {}, {}, {}
        for g in range(F_PASSES):
            for h in range(K_PASSES):
                b_raw[g, h] = keep.tile([P, SLOTS, PASS], BF16, name="b_raw%d%d" % (g, h), align_bytes=64)
                b_codes[g, h] = keep.tile([P, PASS], U32, name="b_codes%d%d" % (g, h), align_bytes=64)
                b_sc[g, h] = keep.tile([P, PASS], U8, name="b_sc%d%d" % (g, h), align_bytes=64)
        h_codes, h_sc = {}, {}
        for r in range(len(RANGES)):
            for g in range(F_PASSES):
                h_codes[r, g] = keep.tile([P, WIDE], U32, name="h_codes%d%d" % (r, g), align_bytes=64)
                h_sc[r, g] = keep.tile([P, WIDE], U8, name="h_sc%d%d" % (r, g), align_bytes=64)
        y_codes = [keep.tile([P, S], U32, name="y_codes%d" % h, align_bytes=64) for h in range(K_PASSES)]
        y_sc = [keep.tile([P, S], U8, name="y_sc%d" % h, align_bytes=64) for h in range(K_PASSES)]
        relay_rows = keep.tile([P, F_PASSES * P], BF16, name="relay_rows", align_bytes=64)
        relay_sb = keep.tile([P, F_PASSES, SLOTS], F32, name="relay_sb", align_bytes=64)
        value_all = keep.tile([P, K], BF16, name="value_all", align_bytes=64)
        ident_bf = keep.tile([P, P], BF16, name="ident_bf", align_bytes=64)
        ident_f32 = keep.tile([P, P], F32, name="ident_f32", align_bytes=64)

        acc, h_pairs, h_bf, b_int, y_f32, y_bf, y_tp, y_t = {}, {}, {}, {}, {}, {}, {}, {}

        def load_scale_rows(plane, rows):
            for quad in range(4):
                nc.sync.dma_start(
                    out=plane[32 * quad : 32 * quad + 4, :, :].bitcast(I32),
                    in_=rows[:, 4 * quad : 4 * quad + 4, :].rearrange("g r n -> r g n").bitcast(I32),
                )

        def load_x(c):
            lo, hi = RANGES[c]
            src = x_words.rearrange("g p n t -> p g (n t)").bitcast(I32)
            nc.sync.dma_start(out=x_codes[c][:].bitcast(I32), in_=src[:, :, lo:hi])

        def load_a(c):
            lo, hi = A_CHUNKS[c]
            src = a_words[:, :, 2 * PASS * lo : 2 * PASS * hi].rearrange("g p n -> p g n")
            nc.sync.dma_start(out=a_raw[c][:].bitcast(I32), in_=src.bitcast(I32))

        def load_b(g, h):
            rows = b[PASS * g : PASS * (g + 1), PASS * h : PASS * (h + 1)].rearrange("(q t r) n -> t q r n", t=SLOTS, r=RUN)
            for t in range(SLOTS):
                nc.sync.dma_start(out=b_raw[g, h][:, t, :], in_=rows[t])

        def setup():
            nc.vector.memset(relay_rows[:], 0.0)
            nc.vector.memset(a_sc_raw[:].bitcast(I32), 0)
            nc.vector.memset(x_sc[:].bitcast(I32), 0)
            nc.scalar.dma_start(
                out=relay_rows[0:SLOTS, :].rearrange("t (a r) -> t a r", r=RUN),
                in_=relay.rearrange("(a t r) -> t a r", t=SLOTS, r=RUN),
            )
            make_identity(nc, ident_bf[:])
            nc.scalar.copy(out=ident_f32[:], in_=ident_bf[:])

        def load(kind, *at):
            if kind == "a":
                load_a(*at)
            elif kind == "x":
                load_x(*at)
            elif kind == "b":
                load_b(*at)
            elif kind == "asc":
                load_scale_rows(a_sc_raw, a_scales)
            elif kind == "xsc":
                load_scale_rows(x_sc, x_scales)
            else:
                nc.sync.dma_start(out=value_all[:], in_=value.partition_broadcast(P))

        def turn_relay():
            turned = psum.tile([P, F_PASSES, P], BF16, name="turned", tag="tp", bufs=2)
            for g in range(F_PASSES):
                nc.tensor.transpose(turned[:, g, :], relay_rows[:, P * g : P * (g + 1)], ident_bf[:])
            nc.scalar.copy(out=relay_sb[:], in_=turned[:, :, 0:SLOTS])

        def perm(g):
            c = [i for i, (lo, hi) in enumerate(A_CHUNKS) if lo <= g < hi][0]
            for dst, src, per_col, at in ((a_codes[g], a_raw[c], 2, g - A_CHUNKS[c][0]), (a_sc[g], a_sc_raw, 1, g)):
                w = RUN * per_col // 4
                nc.vector.tensor_copy(
                    out=dst[:].bitcast(I32).rearrange("p k (t q w) -> p k t q w", t=SLOTS, w=w),
                    in_=src[:, :, per_col * PASS * at : per_col * PASS * (at + 1)].bitcast(I32).rearrange("p k (q t w) -> p k t q w", t=SLOTS, w=w),
                )

        def s1(r, g, j):
            if j > 0:
                return
            for i in range(WIDE // P):
                acc[r, g, i, 1] = psum.tile([P, SLOTS, P], F32, name="acc1", tag="acc", bufs=6)
            for t in range(SLOTS):
                for k in range(K_PASSES):
                    for i in range(WIDE // P):
                        off = P * i
                        nc.tensor.matmul_mx(
                            out=acc[r, g, i, 1][:, t, :],
                            lhsT=a_codes[g][:, k, 2 * P * t : 2 * P * (t + 1)].bitcast(FP4X4),
                            lhsT_scale=a_sc[g][:, k, P * t : P * (t + 1)],
                            rhs=x_codes[r][:, k, off : off + P].bitcast(FP8X4),
                            rhs_scale=x_sc[:, k, WIDE * r + off : WIDE * r + off + P],
                            start=(k == 0),
                            stop=(k == K_PASSES - 1),
                        )

        def hev(r, g, i):
            if i == 0:
                h_pairs[r, g] = work.tile([P, SLOTS * WIDE], BF16, name="h_pairs", tag="h_pairs", bufs=4, align_bytes=64)
            for u in range(2):
                at = 2 * (WIDE * u + P * i)
                nc.vector.scalar_tensor_tensor(
                    out=h_pairs[r, g][:, at : at + 2 * P].rearrange("p (s e) -> p s e", e=2),
                    in0=acc[r, g, i, 1][:, 2 * u : 2 * u + 2, :].rearrange("p e s -> p s e"),
                    scalar=1.0,
                    in1=relay_sb[:, g : g + 1, 2 * u : 2 * u + 2].to_broadcast([P, P, 2]),
                    op0=MIN,
                    op1=MULT,
                )

        def hi(r, g):
            tile_bf = work.tile([P, SLOTS * WIDE], BF16, name="h_bf", tag="h_bf", bufs=5, align_bytes=64)
            h_bf[r, g] = tile_bf
            nc.scalar.copy(
                out=tile_bf[:].bitcast(F32).rearrange("p (s u) -> p s u", u=2),
                in_=h_pairs[r, g][:].bitcast(F32).rearrange("p (u s) -> p s u", u=2),
            )

        def hq(r, g):
            nc.vector.quantize_mx(out=h_codes[r, g][:].bitcast(FP8X4), scales=h_sc[r, g][:], in_=h_bf[r, g][:])

        def bi(g, h):
            tile_bf = work.tile([P, PASS, SLOTS], BF16, name="b_int", tag="b_int", bufs=6, align_bytes=64)
            b_int[g, h] = tile_bf
            nc.scalar.copy(
                out=tile_bf[:].rearrange("p (c i) t -> p c t i", i=4),
                in_=b_raw[g, h][:].rearrange("p t (c i) -> p c t i", i=4),
            )

        def bq(g, h):
            nc.vector.quantize_mx(
                out=b_codes[g, h][:].bitcast(FP8X4), scales=b_sc[g, h][:], in_=b_int[g, h][:].rearrange("p n t -> p (n t)")
            )

        def s2(s, h):
            bank = psum.tile([P, PASS], F32, name="acc2", tag="acc", bufs=6)
            acc[s, h, 2] = bank
            r, off = divmod(P * s, WIDE)
            for g in range(F_PASSES):
                nc.tensor.matmul_mx(
                    out=bank[:],
                    lhsT=h_codes[r, g][:, off : off + P].bitcast(FP8X4),
                    lhsT_scale=h_sc[r, g][:, off : off + P],
                    rhs=b_codes[g, h][:].bitcast(FP8X4),
                    rhs_scale=b_sc[g, h][:],
                    start=(g == 0),
                    stop=(g == F_PASSES - 1),
                )

        def yev(s, h, last):
            cols = slice(PASS * h, PASS * (h + 1))
            y32 = work.tile([P, PASS], F32, name="y32", tag="y32", bufs=6, align_bytes=64)
            tile_bf = work.tile([P, PASS], BF16, name="y_bf", tag="y_bf", bufs=8, align_bytes=64)
            y_bf[s, h] = tile_bf
            sorted_bf = tile_bf[:].rearrange("s (u p e) -> s u p e", u=2, e=2)
            if last:
                sums = acc[s, h, 2][:].rearrange("s (p u e) -> s u p e", u=2, e=2)
                gains = value_all[:, cols].rearrange("s (p u e) -> s u p e", u=2, e=2)
                for u in range(2):
                    nc.vector.scalar_tensor_tensor(
                        out=sorted_bf[:, u], in0=sums[:, u], scalar=1.0, in1=gains[:, u], op0=MIN, op1=MULT
                    )
            nc.vector.scalar_tensor_tensor(
                out=y32[:], in0=acc[s, h, 2][:], scalar=1.0, in1=value_all[:, cols], op0=MIN, op1=MULT
            )
            y_f32[s, h] = y32
            nc.sync.dma_start(out=out_0[P * s : P * (s + 1), cols], in_=y32[:])

        def cast(s, h):
            nc.scalar.copy(
                out=y_bf[s, h][:].rearrange("s (u p e) -> s u p e", u=2, e=2),
                in_=y_f32[s, h][:].rearrange("s (p u e) -> s u p e", u=2, e=2),
            )

        def tp(tiles, h):
            if len(tiles) == 2:
                bank = psum.tile([P, 2, 2, P], F32, name="turned", tag="tp", bufs=2)
            else:
                bank = psum.tile([P, 1, 2, P], F32, name="turned_last", tag="acc", bufs=6)
            y_tp[tiles, h] = bank
            for i, s in enumerate(tiles):
                words = y_bf[s, h][:].bitcast(F32)
                for u in range(2):
                    nc.tensor.transpose(bank[:, i, u, :], words[:, P * u : P * (u + 1)], ident_f32[:])

        def tev(tiles, h):
            tile_bf = work.tile([P, len(tiles) * PASS], BF16, name="y_t", tag="y_t", bufs=4, align_bytes=64)
            y_t[tiles, h] = tile_bf
            nc.scalar.copy(
                out=tile_bf[:].bitcast(F32).rearrange("p (i s u) -> p i s u", s=P, u=2),
                in_=y_tp[tiles, h][:].rearrange("p i u s -> p i s u"),
            )

        def yq(tiles, h):
            cols = slice(P * tiles[0], P * (tiles[-1] + 1))
            nc.vector.quantize_mx(out=y_codes[h][:, cols].bitcast(FP8X4), scales=y_sc[h][:, cols], in_=y_t[tiles, h][:])
            words = out_1[h].rearrange("p m t -> p (m t)").bitcast(I32)
            nc.sync.dma_start(out=words[:, cols], in_=y_codes[h][:, cols].bitcast(I32))
            if tiles[-1] == S_TILES - 1:
                for quad in range(4):
                    nc.sync.dma_start(
                        out=out_2[h, 4 * quad : 4 * quad + 4, :].bitcast(I32),
                        in_=y_sc[h][32 * quad : 32 * quad + 4, :].bitcast(I32),
                    )

        pipeline(
            {
                "setup": setup, "load": load, "hi": hi, "cast": cast, "relay": turn_relay, "perm": perm, "bi": bi, "bq": bq, "s1": s1, "hev": hev, "hq": hq,
                "s2": s2, "yev": yev, "tp": tp, "tev": tev, "yq": yq,
            }
        )
